import numpy as np
import ml_dtypes


def mxq(x, axis, fmt="e4m3"):
    dtype, down = {"e4m3": (ml_dtypes.float8_e4m3fn, 7), "e5m2": (ml_dtypes.float8_e5m2, 14)}[fmt]
    v = np.moveaxis(np.asarray(x, np.float32).astype(ml_dtypes.bfloat16).astype(np.float64), axis, -1)
    blocks = v.reshape(v.shape[:-1] + (-1, 32))
    amax = np.abs(blocks).max(-1, keepdims=True)
    byte = np.maximum(np.where(amax > 0, np.frexp(amax)[1] - 1 + 127, 0) - down, 1)
    scale = np.exp2(byte - 127.0)
    codes = (blocks / scale).astype(np.float32).astype(dtype).astype(np.float64)
    return np.moveaxis((codes * scale).reshape(v.shape), -1, axis)


WIDE = False


def mx_kscale(k):
    if not WIDE:
        return np.ones(k)
    levels = np.array([10, -10, 5, -5, 0])
    if k % 512:
        return np.exp2(np.random.permutation(np.resize(levels, k // 32))).repeat(32)
    a = np.empty((k // 512, 16))
    for p in range(k // 512):
        a[p, :8] = np.random.permutation(np.resize(levels, 8))
        for g in range(8):
            far = levels[np.abs(levels - a[p, g]) >= 10]
            a[p, g + 8] = far[np.random.randint(len(far))]
    return np.exp2(a.ravel()).repeat(32)


def f64(x):
    return np.asarray(x).astype(np.float64)


def striped(idx):
    return np.tile(np.asarray(idx).reshape(-1, 16).T, (8, 1)).astype(np.uint16)


def unstriped(offs):
    return offs[:16].T.reshape(-1).astype(np.int64)


E2M1 = np.array([0.0, 0.5, 1.0, 1.5, 2.0, 3.0, 4.0, 6.0, -0.0, -0.5, -1.0, -1.5, -2.0, -3.0, -4.0, -6.0])


def pack_weight(w, fmt):
    k, n = w.shape
    w = f64(np.asarray(w, np.float32).astype(ml_dtypes.bfloat16)).reshape(k // 32, 32, n)
    amax = np.abs(w).max(1)
    if fmt == "e4m3":
        byte = np.frexp(amax)[1] - 1 + 127 - 7
    else:
        mant, ex = np.frexp(amax / 6.0)
        byte = np.where(mant > 0.5, ex, ex - 1) + 127
    byte = np.clip(np.where(amax > 0, byte, 1), 1, 254)
    scaled = (w * np.exp2(127.0 - byte)[:, None, :]).reshape(k, n).astype(np.float32)
    by_word = np.ascontiguousarray(scaled.reshape(k // 512, 128, 4, n).transpose(0, 1, 3, 2))
    if fmt == "e4m3":
        words = by_word.astype(ml_dtypes.float8_e4m3fn).view(np.uint8)
    else:
        c = by_word.astype(ml_dtypes.float4_e2m1fn).view(np.uint8) & 0xF
        words = (c[..., 0::2] | (c[..., 1::2] << 4)).reshape(k // 512, 128, 2 * n)
    return np.ascontiguousarray(words), np.ascontiguousarray(byte.astype(np.uint8).reshape(k // 512, 16, n))


def unpack_weight(words, scales, fmt):
    g, _, n = scales.shape
    words = np.ascontiguousarray(words).reshape(g, 128, n, -1)
    if fmt == "e4m3":
        vals = words.view(ml_dtypes.float8_e4m3fn).astype(np.float64)
    else:
        nib = np.empty((g, 128, n, 4), np.uint8)
        nib[..., 0::2] = words & 0xF
        nib[..., 1::2] = words >> 4
        vals = E2M1[nib]
    vals = vals * np.repeat(np.exp2(scales.astype(np.float64) - 127.0), 8, axis=1)[..., None]
    return vals.transpose(0, 1, 3, 2).reshape(g * 512, n)


K, T, I, P, Q, G = 512, 4096, 1024, 512, 256, 64


def setup_inputs():
    n = np.random.standard_normal
    idx = (np.random.permutation(T // 16)[:I // 16, None] * 16 + np.arange(16)).reshape(-1)
    fk = mx_kscale(K)
    fp = mx_kscale(P)
    embp = pack_weight(n((K, T)) / fk[:, None], "e2m1")
    return {
        "emb_words": embp[0],
        "emb_scales": embp[1],
        "wp": (n((K, P)) * 1 / np.sqrt(K) * fk[:, None] / fp).astype(np.float32),
        "qt": (n((P, Q)) * 1.0 / np.sqrt(P) * fp[:, None]).astype(np.float32),
        "offs": striped(idx),
    }


def reference(emb_words, emb_scales, wp, qt, offs):
    idx = unstriped(offs)
    embu = unpack_weight(emb_words, emb_scales, "e2m1")
    wpq = mxq(f64(wp), 0, "e4m3")
    embidxg = embu[:, idx]
    dt = wpq.T @ embidxg
    qtq = mxq(f64(qt), 0, "e4m3")
    dtq = mxq(dt, 0, "e4m3")
    a = qtq.T @ dtq
    y = a.reshape(Q, G, I // G).max(axis=2)
    return y

@@ -1,0 +1,171 @@
+from contextlib import ExitStack
+
+import concourse.mybir as mybir
+
+K, T, SLOTS, PROJ, Q, G = 512, 4096, 1024, 512, 256, 64
+FLOPS = 2 * K * PROJ * SLOTS + 2 * PROJ * Q * SLOTS
+
+F32 = mybir.dt.float32
+BF16 = mybir.dt.bfloat16
+I32 = mybir.dt.int32
+U32 = mybir.dt.uint32
+U16 = mybir.dt.uint16
+U8 = mybir.dt.uint8
+FP8X4 = mybir.dt.float8_e4m3fn_x4
+FP4X4 = mybir.dt.float4_e2m1fn_x4
+
+P = 128
+PACK = 4
+CHUNK = 128
+RUN = 16
+
+
+def tile_attend_colbert_proj_kernel(tc, emb_words, emb_scales, wp, qt, offs, out):
+    nc = tc.nc
+    with ExitStack() as ctx:
+        keep = ctx.enter_context(tc.tile_pool(name="keep", bufs=1))
+        proj_banks = ctx.enter_context(tc.psum_pool(name="proj_banks", bufs=6))
+        score_banks = ctx.enter_context(tc.psum_pool(name="score_banks", bufs=2))
+
+        offsets = keep.tile([P, SLOTS // 16], U16, name="offsets")
+        pool_words = keep.tile([P, T], U16, name="pool_words", align_bytes=64)
+        pool_scales = keep.tile([P, T], U8, name="pool_scales", align_bytes=64)
+        nc.vector.memset(pool_scales[:].bitcast(I32), 0)
+        nc.sync.dma_start(offsets[:], offs)
+        for r in range(4):
+            nc.sync.dma_start(pool_scales[r:P:32, :].bitcast(I32), emb_scales[0, r:16:4, :].bitcast(I32))
+        nc.sync.dma_start(pool_words[:].bitcast(I32), emb_words[0].bitcast(I32))
+        wp_rows = wp.rearrange("(p j) c -> p j c", j=PACK)
+        wp_raw = [keep.tile([P, PACK, PROJ // 2], F32, name="wp_raw%d" % u) for u in range(2)]
+        for u in range(2):
+            nc.sync.dma_start(wp_raw[u][:], wp_rows[:, :, u * 256 : (u + 1) * 256])
+        qt_raw = keep.tile([P, PACK, Q], F32, name="qt_raw")
+        nc.sync.dma_start(qt_raw[:], qt.rearrange("(p j) q -> p j q", j=PACK))
+
+        slot_scales = keep.tile([P, SLOTS], U8, name="slot_scales", align_bytes=64)
+        slot_words = [keep.tile([P, SLOTS // 2], U16, name="slot_words%d" % h, align_bytes=64) for h in range(2)]
+        wp_bf = keep.tile([P, PACK * P * PACK], BF16, name="wp_bf", align_bytes=64)
+        wp_codes = keep.tile([P, PROJ], U32, name="wp_codes", align_bytes=64)
+        wp_scales = keep.tile([P, PROJ], U8, name="wp_scales", align_bytes=64)
+        qt_bf = keep.tile([P, Q * PACK], BF16, name="qt_bf", align_bytes=64)
+        qt_codes = keep.tile([P, Q], U32, name="qt_codes", align_bytes=64)
+        qt_scales = keep.tile([P, Q], U8, name="qt_scales", align_bytes=64)
+        dt_bf = keep.tile([P, SLOTS * PACK], BF16, name="dt_bf", align_bytes=64)
+        dt_codes = keep.tile([P, SLOTS], U32, name="dt_codes", align_bytes=64)
+        dt_scales = keep.tile([P, SLOTS], U8, name="dt_scales", align_bytes=64)
+        best = keep.tile([P, 2, G], F32, name="best")
+
+        def copy_on(engine, dst, src):
+            if engine == "scalar":
+                nc.scalar.copy(dst, src)
+            elif engine == "gpsimd":
+                nc.gpsimd.tensor_scalar(dst, src, 1.0, 0.0, mybir.AluOpType.mult, mybir.AluOpType.add)
+            else:
+                nc.vector.tensor_copy(dst, src)
+
+        def gather_scales(a, b):
+            nc.vector.tensor_copy(slot_scales[:, a:b], pool_scales[:].indirect(offsets[:, a // 16 : b // 16]))
+
+        def gather_words(h):
+            nc.vector.tensor_copy(slot_words[h][:], pool_words[:].indirect(offsets[:, 32 * h : 32 * (h + 1)]))
+
+        def round_wp(engine, piece, m0, m1):
+            base = piece * (P // len(wp_raw))
+            dst = wp_bf[:].rearrange("p (t m j) -> p m j t", t=PACK, j=PACK)[:, base + m0 : base + m1]
+            src = wp_raw[piece][:].rearrange("p j (m t) -> p m j t", t=PACK)[:, m0:m1]
+            copy_on(engine, dst, src)
+
+        def quantize(codes, scales, values, a, b):
+            nc.vector.quantize_mx(out=codes[:, a:b].bitcast(FP8X4), scales=scales[:, a:b], in_=values[:, PACK * a : PACK * b])
+
+        def round_qt(engine, m0, m1):
+            dst = qt_bf[:].rearrange("p (h m j) -> p m j h", h=2, j=PACK)[:, m0:m1]
+            src = qt_raw[:].rearrange("p j (m h) -> p m j h", h=2)[:, m0:m1]
+            copy_on(engine, dst, src)
+
+        banks = {}
+
+        def project(c):
+            bank = proj_banks.tile([P, PACK, CHUNK], F32, name="bank")
+            banks[c] = bank
+            h, lo = divmod(c * CHUNK, SLOTS // 2)
+            for t in range(PACK):
+                nc.tensor.matmul_mx(
+                    out=bank[:, t, :],
+                    lhsT=wp_codes[:, t * P : (t + 1) * P].bitcast(FP8X4),
+                    lhsT_scale=wp_scales[:, t * P : (t + 1) * P],
+                    rhs=slot_words[h][:, lo : lo + CHUNK].bitcast(FP4X4),
+                    rhs_scale=slot_scales[:, c * CHUNK : (c + 1) * CHUNK],
+                    start=True,
+                    stop=True,
+                )
+
+        def round_dt(engine, c):
+            dst = dt_bf[:, c * CHUNK * PACK : (c + 1) * CHUNK * PACK].rearrange("p (n t) -> p n t", t=PACK)
+            copy_on(engine, dst, banks[c][:].rearrange("p t n -> p n t"))
+
+        scores = {}
+
+        def score(a, b):
+            bank = score_banks.tile([P, 2, b - a], F32, name="score")
+            scores[a] = bank
+            for h in range(2):
+                nc.tensor.matmul_mx(
+                    out=bank[:, h, :],
+                    lhsT=qt_codes[:, h * P : (h + 1) * P].bitcast(FP8X4),
+                    lhsT_scale=qt_scales[:, h * P : (h + 1) * P],
+                    rhs=dt_codes[:, a:b].bitcast(FP8X4),
+                    rhs_scale=dt_scales[:, a:b],
+                    start=True,
+                    stop=True,
+                )
+
+        def keep_best(a, b):
+            nc.vector.tensor_reduce(
+                best[:, :, a // RUN : b // RUN],
+                scores[a][:].rearrange("p h (g s) -> p h g s", s=RUN),
+                mybir.AxisListType.X,
+                mybir.AluOpType.max,
+            )
+
+        def qd(a, b):
+            quantize(dt_codes, dt_scales, dt_bf, a, b)
+
+        gather_scales(0, 1024)
+        gather_words(0)
+        round_wp("scalar", 0, 0, 64)
+        gather_words(1)
+        round_wp("scalar", 1, 0, 24)
+        round_wp("vector", 1, 24, 64)
+        quantize(wp_codes, wp_scales, wp_bf, 0, 256)
+        quantize(wp_codes, wp_scales, wp_bf, 256, 512)
+        for c in range(6):
+            project(c)
+        round_qt("vector", 0, 128)
+        round_dt("scalar", 0)
+        quantize(qt_codes, qt_scales, qt_bf, 0, 256)
+        round_dt("vector", 1)
+        round_dt("scalar", 2)
+        project(6)
+        project(7)
+        qd(0, 256)
+        round_dt("scalar", 3)
+        score(0, 256)
+        round_dt("scalar", 4)
+        qd(256, 512)
+        keep_best(0, 256)
+        score(256, 512)
+        round_dt("scalar", 5)
+        keep_best(256, 512)
+        round_dt("scalar", 6)
+        qd(512, 768)
+        score(512, 768)
+        round_dt("scalar", 7)
+        qd(768, 896)
+        keep_best(512, 768)
+        score(768, 896)
+        qd(896, 1024)
+        keep_best(768, 896)
+        score(896, 1024)
+        keep_best(896, 1024)
+        nc.sync.dma_start(out.rearrange("(p h) g -> p h g", h=2), best[:])

@@ -24,27 +24,28 @@ def tile_attend_colbert_proj_kernel(tc, emb_words, emb_scales, wp, qt, offs, out
     nc = tc.nc
     with ExitStack() as ctx:
         keep = ctx.enter_context(tc.tile_pool(name="keep", bufs=1))
-        proj_banks = ctx.enter_context(tc.psum_pool(name="proj_banks", bufs=6))
-        score_banks = ctx.enter_context(tc.psum_pool(name="score_banks", bufs=2))
+        proj_banks = ctx.enter_context(tc.psum_pool(name="proj_banks", bufs=4))
+        score_banks = ctx.enter_context(tc.psum_pool(name="score_banks", bufs=4))
 
         offsets = keep.tile([P, SLOTS // 16], U16, name="offsets")
         pool_words = keep.tile([P, T], U16, name="pool_words", align_bytes=64)
         pool_scales = keep.tile([P, T], U8, name="pool_scales", align_bytes=64)
         nc.vector.memset(pool_scales[:].bitcast(I32), 0)
         nc.sync.dma_start(offsets[:], offs)
+        wp_rows = wp.rearrange("(p j) c -> p j c", j=PACK)
+        wp_raw = [keep.tile([P, PACK, PROJ // 2], F32, name="wp_raw%d" % u) for u in range(2)]
+        nc.sync.dma_start(wp_raw[0][:], wp_rows[:, :, 0:256])
+        for j0, j1 in ((0, 1), (1, 2), (2, 4)):
+            nc.sync.dma_start(wp_raw[1][:, j0:j1, :], wp_rows[:, j0:j1, 256:512])
         for r in range(4):
             nc.sync.dma_start(pool_scales[r:P:32, :].bitcast(I32), emb_scales[0, r:16:4, :].bitcast(I32))
         nc.sync.dma_start(pool_words[:].bitcast(I32), emb_words[0].bitcast(I32))
-        wp_rows = wp.rearrange("(p j) c -> p j c", j=PACK)
-        wp_raw = [keep.tile([P, PACK, PROJ // 2], F32, name="wp_raw%d" % u) for u in range(2)]
-        for u in range(2):
-            nc.sync.dma_start(wp_raw[u][:], wp_rows[:, :, u * 256 : (u + 1) * 256])
         qt_raw = keep.tile([P, PACK, Q], F32, name="qt_raw")
         nc.sync.dma_start(qt_raw[:], qt.rearrange("(p j) q -> p j q", j=PACK))
 
-        slot_scales = keep.tile([P, SLOTS], U8, name="slot_scales", align_bytes=64)
+        held = {}
         slot_words = [keep.tile([P, SLOTS // 2], U16, name="slot_words%d" % h, align_bytes=64) for h in range(2)]
-        wp_bf = keep.tile([P, PACK * P * PACK], BF16, name="wp_bf", align_bytes=64)
+        wp_bf = keep.tile([P, PACK * P * PACK], BF16, name="wp_bf", tag="reused", align_bytes=64)
         wp_codes = keep.tile([P, PROJ], U32, name="wp_codes", align_bytes=64)
         wp_scales = keep.tile([P, PROJ], U8, name="wp_scales", align_bytes=64)
         qt_bf = keep.tile([P, Q * PACK], BF16, name="qt_bf", align_bytes=64)
@@ -63,8 +64,9 @@ def tile_attend_colbert_proj_kernel(tc, emb_words, emb_scales, wp, qt, offs, out
             else:
                 nc.vector.tensor_copy(dst, src)
 
-        def gather_scales(a, b):
-            nc.vector.tensor_copy(slot_scales[:, a:b], pool_scales[:].indirect(offsets[:, a // 16 : b // 16]))
+        def gather_scales():
+            held["scales"] = keep.tile([P, SLOTS], U8, name="slot_scales", tag="reused", align_bytes=64)
+            nc.vector.tensor_copy(held["scales"][:], pool_scales[:].indirect(offsets[:]))
 
         def gather_words(h):
             nc.vector.tensor_copy(slot_words[h][:], pool_words[:].indirect(offsets[:, 32 * h : 32 * (h + 1)]))
@@ -79,8 +81,8 @@ def tile_attend_colbert_proj_kernel(tc, emb_words, emb_scales, wp, qt, offs, out
             nc.vector.quantize_mx(out=codes[:, a:b].bitcast(FP8X4), scales=scales[:, a:b], in_=values[:, PACK * a : PACK * b])
 
         def round_qt(engine, m0, m1):
-            dst = qt_bf[:].rearrange("p (h m j) -> p m j h", h=2, j=PACK)[:, m0:m1]
-            src = qt_raw[:].rearrange("p j (m h) -> p m j h", h=2)[:, m0:m1]
+            dst = qt_bf[:].rearrange("p (h c u j) -> p c j u h", h=2, u=2, j=PACK)[:, m0:m1]
+            src = qt_raw[:].rearrange("p j (c u h) -> p c j u h", u=2, h=2)[:, m0:m1]
             copy_on(engine, dst, src)
 
         banks = {}
@@ -95,7 +97,7 @@ def tile_attend_colbert_proj_kernel(tc, emb_words, emb_scales, wp, qt, offs, out
                     lhsT=wp_codes[:, t * P : (t + 1) * P].bitcast(FP8X4),
                     lhsT_scale=wp_scales[:, t * P : (t + 1) * P],
                     rhs=slot_words[h][:, lo : lo + CHUNK].bitcast(FP4X4),
-                    rhs_scale=slot_scales[:, c * CHUNK : (c + 1) * CHUNK],
+                    rhs_scale=held["scales"][:, c * CHUNK : (c + 1) * CHUNK],
                     start=True,
                     stop=True,
                 )
@@ -131,41 +133,43 @@ def tile_attend_colbert_proj_kernel(tc, emb_words, emb_scales, wp, qt, offs, out
         def qd(a, b):
             quantize(dt_codes, dt_scales, dt_bf, a, b)
 
-        gather_scales(0, 1024)
-        gather_words(0)
-        round_wp("scalar", 0, 0, 64)
-        gather_words(1)
+        round_wp("scalar", 0, 0, 24)
+        round_wp("vector", 0, 24, 64)
         round_wp("scalar", 1, 0, 24)
         round_wp("vector", 1, 24, 64)
-        quantize(wp_codes, wp_scales, wp_bf, 0, 256)
-        quantize(wp_codes, wp_scales, wp_bf, 256, 512)
-        for c in range(6):
+        quantize(wp_codes, wp_scales, wp_bf, 0, 512)
+        gather_scales()
+        gather_words(0)
+        gather_words(1)
+        for c in range(4):
             project(c)
-        round_qt("vector", 0, 128)
-        round_dt("scalar", 0)
+        round_qt("vector", 0, 64)
         quantize(qt_codes, qt_scales, qt_bf, 0, 256)
-        round_dt("vector", 1)
+        round_dt("scalar", 0)
+        project(4)
+        round_dt("scalar", 1)
+        project(5)
+        qd(0, 256)
         round_dt("scalar", 2)
         project(6)
-        project(7)
-        qd(0, 256)
-        round_dt("scalar", 3)
         score(0, 256)
-        round_dt("scalar", 4)
+        round_dt("scalar", 3)
+        project(7)
         qd(256, 512)
         keep_best(0, 256)
         score(256, 512)
+        round_dt("scalar", 4)
         round_dt("scalar", 5)
-        keep_best(256, 512)
-        round_dt("scalar", 6)
         qd(512, 768)
+        keep_best(256, 512)
         score(512, 768)
-        round_dt("scalar", 7)
+        round_dt("scalar", 6)
         qd(768, 896)
-        keep_best(512, 768)
+        round_dt("scalar", 7)
         score(768, 896)
         qd(896, 1024)
-        keep_best(768, 896)
+        keep_best(512, 768)
         score(896, 1024)
+        keep_best(768, 896)
         keep_best(896, 1024)
         nc.sync.dma_start(out.rearrange("(p h) g -> p h g", h=2), best[:])

@@ -29,23 +29,25 @@ def tile_attend_colbert_proj_kernel(tc, emb_words, emb_scales, wp, qt, offs, out
 
         offsets = keep.tile([P, SLOTS // 16], U16, name="offsets")
         pool_words = keep.tile([P, T], U16, name="pool_words", align_bytes=64)
-        pool_scales = keep.tile([P, T], U8, name="pool_scales", align_bytes=64)
-        nc.vector.memset(pool_scales[:].bitcast(I32), 0)
+        pool_scales = keep.tile([P, T], U8, name="pool_scales", tag="window", align_bytes=64)
+        slot_scales = keep.tile([P, SLOTS], U8, name="slot_scales", align_bytes=64)
+        plane = keep.tile([P, SLOTS], U8, name="plane", align_bytes=64)
+        nc.vector.memset(pool_scales[0:112, :].bitcast(I32), 0)
+        nc.vector.memset(plane[:].bitcast(I32), 0)
         nc.sync.dma_start(offsets[:], offs)
+        nc.sync.dma_start(pool_scales[112:P, :].bitcast(I32), emb_scales[0].bitcast(I32))
         wp_rows = wp.rearrange("(p j) c -> p j c", j=PACK)
-        wp_raw = [keep.tile([P, PACK, PROJ // 2], F32, name="wp_raw%d" % u) for u in range(2)]
-        nc.sync.dma_start(wp_raw[0][:], wp_rows[:, :, 0:256])
-        for j0, j1 in ((0, 1), (1, 2), (2, 4)):
-            nc.sync.dma_start(wp_raw[1][:, j0:j1, :], wp_rows[:, j0:j1, 256:512])
-        for r in range(4):
-            nc.sync.dma_start(pool_scales[r:P:32, :].bitcast(I32), emb_scales[0, r:16:4, :].bitcast(I32))
+        wp_raw = keep.tile([P, PACK, PROJ], F32, name="wp_raw")
+        nc.sync.dma_start(wp_raw[:], wp_rows)
         nc.sync.dma_start(pool_words[:].bitcast(I32), emb_words[0].bitcast(I32))
-        qt_raw = keep.tile([P, PACK, Q], F32, name="qt_raw")
+        nc.vector.tensor_copy(slot_scales[:], pool_scales[:].indirect(offsets[:]))
+        for r in range(4):
+            nc.sync.dma_start(plane[r:P:32, :].bitcast(I32), slot_scales[112 + r : P : 4, :].bitcast(I32))
+        qt_raw = keep.tile([P, PACK, Q], F32, name="qt_raw", tag="window", align_bytes=64)
         nc.sync.dma_start(qt_raw[:], qt.rearrange("(p j) q -> p j q", j=PACK))
 
-        held = {}
         slot_words = [keep.tile([P, SLOTS // 2], U16, name="slot_words%d" % h, align_bytes=64) for h in range(2)]
-        wp_bf = keep.tile([P, PACK * P * PACK], BF16, name="wp_bf", tag="reused", align_bytes=64)
+        wp_bf = keep.tile([P, PACK * P * PACK], BF16, name="wp_bf", align_bytes=64)
         wp_codes = keep.tile([P, PROJ], U32, name="wp_codes", align_bytes=64)
         wp_scales = keep.tile([P, PROJ], U8, name="wp_scales", align_bytes=64)
         qt_bf = keep.tile([P, Q * PACK], BF16, name="qt_bf", align_bytes=64)
@@ -64,17 +66,12 @@ def tile_attend_colbert_proj_kernel(tc, emb_words, emb_scales, wp, qt, offs, out
             else:
                 nc.vector.tensor_copy(dst, src)
 
-        def gather_scales():
-            held["scales"] = keep.tile([P, SLOTS], U8, name="slot_scales", tag="reused", align_bytes=64)
-            nc.vector.tensor_copy(held["scales"][:], pool_scales[:].indirect(offsets[:]))
-
         def gather_words(h):
             nc.vector.tensor_copy(slot_words[h][:], pool_words[:].indirect(offsets[:, 32 * h : 32 * (h + 1)]))
 
-        def round_wp(engine, piece, m0, m1):
-            base = piece * (P // len(wp_raw))
-            dst = wp_bf[:].rearrange("p (t m j) -> p m j t", t=PACK, j=PACK)[:, base + m0 : base + m1]
-            src = wp_raw[piece][:].rearrange("p j (m t) -> p m j t", t=PACK)[:, m0:m1]
+        def round_wp(engine, m0, m1):
+            dst = wp_bf[:].rearrange("p (t m j) -> p m j t", t=PACK, j=PACK)[:, m0:m1]
+            src = wp_raw[:].rearrange("p j (m t) -> p m j t", t=PACK)[:, m0:m1]
             copy_on(engine, dst, src)
 
         def quantize(codes, scales, values, a, b):
@@ -97,7 +94,7 @@ def tile_attend_colbert_proj_kernel(tc, emb_words, emb_scales, wp, qt, offs, out
                     lhsT=wp_codes[:, t * P : (t + 1) * P].bitcast(FP8X4),
                     lhsT_scale=wp_scales[:, t * P : (t + 1) * P],
                     rhs=slot_words[h][:, lo : lo + CHUNK].bitcast(FP4X4),
-                    rhs_scale=held["scales"][:, c * CHUNK : (c + 1) * CHUNK],
+                    rhs_scale=plane[:, c * CHUNK : (c + 1) * CHUNK],
                     start=True,
                     stop=True,
                 )
@@ -133,12 +130,9 @@ def tile_attend_colbert_proj_kernel(tc, emb_words, emb_scales, wp, qt, offs, out
         def qd(a, b):
             quantize(dt_codes, dt_scales, dt_bf, a, b)
 
-        round_wp("scalar", 0, 0, 24)
-        round_wp("vector", 0, 24, 64)
-        round_wp("scalar", 1, 0, 24)
-        round_wp("vector", 1, 24, 64)
+        round_wp("scalar", 0, 40)
+        round_wp("vector", 40, 128)
         quantize(wp_codes, wp_scales, wp_bf, 0, 512)
-        gather_scales()
         gather_words(0)
         gather_words(1)
         for c in range(4):

@@ -18,18 +18,21 @@ P = 128
 PACK = 4
 CHUNK = 128
 RUN = 16
+STORES = ((0, 2, 6144), (2, 4, 8192), (4, 8, 11264),)
+GROUPS = ((0, 2, 4096), (2, 4, 6144), (4, 6, 8192), (6, 7, 10240), (7, 8, 11264))
 
 
 def tile_attend_colbert_proj_kernel(tc, emb_words, emb_scales, wp, qt, offs, out):
     nc = tc.nc
     with ExitStack() as ctx:
         keep = ctx.enter_context(tc.tile_pool(name="keep", bufs=1))
-        proj_banks = ctx.enter_context(tc.psum_pool(name="proj_banks", bufs=4))
-        score_banks = ctx.enter_context(tc.psum_pool(name="score_banks", bufs=4))
+        shared = ctx.enter_context(tc.tile_pool(name="shared", bufs=1))
+        proj_banks = ctx.enter_context(tc.psum_pool(name="proj_banks", bufs=5))
+        score_banks = ctx.enter_context(tc.psum_pool(name="score_banks", bufs=3))
 
         offsets = keep.tile([P, SLOTS // 16], U16, name="offsets")
         pool_words = keep.tile([P, T], U16, name="pool_words", align_bytes=64)
-        pool_scales = keep.tile([P, T], U8, name="pool_scales", tag="window", align_bytes=64)
+        pool_scales = shared.tile([P, T], U8, name="pool_scales", offset=0, align_bytes=64)
         slot_scales = keep.tile([P, SLOTS], U8, name="slot_scales", align_bytes=64)
         plane = keep.tile([P, SLOTS], U8, name="plane", align_bytes=64)
         nc.vector.memset(pool_scales[0:112, :].bitcast(I32), 0)
@@ -43,20 +46,21 @@ def tile_attend_colbert_proj_kernel(tc, emb_words, emb_scales, wp, qt, offs, out
         nc.vector.tensor_copy(slot_scales[:], pool_scales[:].indirect(offsets[:]))
         for r in range(4):
             nc.sync.dma_start(plane[r:P:32, :].bitcast(I32), slot_scales[112 + r : P : 4, :].bitcast(I32))
-        qt_raw = keep.tile([P, PACK, Q], F32, name="qt_raw", tag="window", align_bytes=64)
+        qt_raw = shared.tile([P, PACK, Q], F32, name="qt_raw", offset=0, align_bytes=64)
         nc.sync.dma_start(qt_raw[:], qt.rearrange("(p j) q -> p j q", j=PACK))
 
-        slot_words = [keep.tile([P, SLOTS // 2], U16, name="slot_words%d" % h, align_bytes=64) for h in range(2)]
-        wp_bf = keep.tile([P, PACK * P * PACK], BF16, name="wp_bf", align_bytes=64)
+        slot_words = {}
+        wp_bf = shared.tile([P, PACK * P * PACK], BF16, name="wp_bf", offset=12288, align_bytes=64)
         wp_codes = keep.tile([P, PROJ], U32, name="wp_codes", align_bytes=64)
         wp_scales = keep.tile([P, PROJ], U8, name="wp_scales", align_bytes=64)
         qt_bf = keep.tile([P, Q * PACK], BF16, name="qt_bf", align_bytes=64)
         qt_codes = keep.tile([P, Q], U32, name="qt_codes", align_bytes=64)
         qt_scales = keep.tile([P, Q], U8, name="qt_scales", align_bytes=64)
-        dt_bf = keep.tile([P, SLOTS * PACK], BF16, name="dt_bf", align_bytes=64)
+        dt_bf = {}
         dt_codes = keep.tile([P, SLOTS], U32, name="dt_codes", align_bytes=64)
         dt_scales = keep.tile([P, SLOTS], U8, name="dt_scales", align_bytes=64)
-        best = keep.tile([P, 2, G], F32, name="best")
+        out_rows = out.rearrange("(p h) g -> p h g", h=2)
+        best = {}
 
         def copy_on(engine, dst, src):
             if engine == "scalar":
@@ -67,6 +71,7 @@ def tile_attend_colbert_proj_kernel(tc, emb_words, emb_scales, wp, qt, offs, out
                 nc.vector.tensor_copy(dst, src)
 
         def gather_words(h):
+            slot_words[h] = shared.tile([P, SLOTS // 2], U16, name="slot_words%d" % h, offset=12288 + SLOTS * h, align_bytes=64)
             nc.vector.tensor_copy(slot_words[h][:], pool_words[:].indirect(offsets[:, 32 * h : 32 * (h + 1)]))
 
         def round_wp(engine, m0, m1):
@@ -100,7 +105,10 @@ def tile_attend_colbert_proj_kernel(tc, emb_words, emb_scales, wp, qt, offs, out
                 )
 
         def round_dt(engine, c):
-            dst = dt_bf[:, c * CHUNK * PACK : (c + 1) * CHUNK * PACK].rearrange("p (n t) -> p n t", t=PACK)
+            first, last, place = [g for g in GROUPS if g[0] <= c < g[1]][0]
+            if first not in dt_bf:
+                dt_bf[first] = shared.tile([P, (last - first) * CHUNK * PACK], BF16, name="dt_bf%d" % first, offset=place, align_bytes=64)
+            dst = dt_bf[first][:, (c - first) * CHUNK * PACK : (c - first + 1) * CHUNK * PACK].rearrange("p (n t) -> p n t", t=PACK)
             copy_on(engine, dst, banks[c][:].rearrange("p t n -> p n t"))
 
         scores = {}
@@ -120,35 +128,54 @@ def tile_attend_colbert_proj_kernel(tc, emb_words, emb_scales, wp, qt, offs, out
                 )
 
         def keep_best(a, b):
+            first, last, place = [g for g in STORES if g[0] * CHUNK <= a < g[1] * CHUNK][0]
+            g0, g1 = first * CHUNK // RUN, last * CHUNK // RUN
+            if first not in best:
+                best[first] = shared.tile([P, 2, g1 - g0], F32, name="best%d" % first, offset=place, align_bytes=64)
             nc.vector.tensor_reduce(
-                best[:, :, a // RUN : b // RUN],
+                best[first][:, :, a // RUN - g0 : b // RUN - g0],
                 scores[a][:].rearrange("p h (g s) -> p h g s", s=RUN),
                 mybir.AxisListType.X,
                 mybir.AluOpType.max,
             )
+            if b == last * CHUNK:
+                nc.sync.dma_start(out_rows[:, :, g0:g1], best[first][:])
 
         def qd(a, b):
-            quantize(dt_codes, dt_scales, dt_bf, a, b)
+            nc.vector.quantize_mx(out=dt_codes[:, a:b].bitcast(FP8X4), scales=dt_scales[:, a:b], in_=dt_bf[a // CHUNK][:])
 
-        round_wp("scalar", 0, 40)
-        round_wp("vector", 40, 128)
+        round_wp("scalar", 0, 32)
+        round_wp("vector", 32, 128)
         quantize(wp_codes, wp_scales, wp_bf, 0, 512)
+        idle_bank = score_banks.tile([P, 2, 256], F32, name="score")
+        for i in range(3):
+            nc.tensor.matmul_mx(
+                out=idle_bank[:].rearrange("p h n -> p (h n)"),
+                lhsT=wp_codes[:, 0:P].bitcast(FP8X4),
+                lhsT_scale=wp_scales[:, 0:P],
+                rhs=wp_codes[:].bitcast(FP8X4),
+                rhs_scale=wp_scales[:],
+                start=True,
+                stop=True,
+            )
         gather_words(0)
         gather_words(1)
-        for c in range(4):
-            project(c)
+        project(0)
+        project(1)
+        project(2)
+        project(3)
+        project(4)
+        round_dt("scalar", 0)
+        project(5)
+        round_dt("vector", 1)
+        project(6)
         round_qt("vector", 0, 64)
         quantize(qt_codes, qt_scales, qt_bf, 0, 256)
-        round_dt("scalar", 0)
-        project(4)
-        round_dt("scalar", 1)
-        project(5)
         qd(0, 256)
         round_dt("scalar", 2)
-        project(6)
+        project(7)
         score(0, 256)
         round_dt("scalar", 3)
-        project(7)
         qd(256, 512)
         keep_best(0, 256)
         score(256, 512)
@@ -159,11 +186,10 @@ def tile_attend_colbert_proj_kernel(tc, emb_words, emb_scales, wp, qt, offs, out
         score(512, 768)
         round_dt("scalar", 6)
         qd(768, 896)
-        round_dt("scalar", 7)
         score(768, 896)
+        round_dt("scalar", 7)
         qd(896, 1024)
         keep_best(512, 768)
         score(896, 1024)
         keep_best(768, 896)
         keep_best(896, 1024)
-        nc.sync.dma_start(out.rearrange("(p h) g -> p h g", h=2), best[:])

@@ -31,7 +31,7 @@ def tile_attend_colbert_proj_kernel(tc, emb_words, emb_scales, wp, qt, offs, out
         score_banks = ctx.enter_context(tc.psum_pool(name="score_banks", bufs=3))
 
         offsets = keep.tile([P, SLOTS // 16], U16, name="offsets")
-        pool_words = keep.tile([P, T], U16, name="pool_words", align_bytes=64)
+        pool_words = shared.tile([P, T], U16, name="pool_words", offset=16384, align_bytes=64)
         pool_scales = shared.tile([P, T], U8, name="pool_scales", offset=0, align_bytes=64)
         slot_scales = keep.tile([P, SLOTS], U8, name="slot_scales", align_bytes=64)
         plane = keep.tile([P, SLOTS], U8, name="plane", align_bytes=64)
@@ -43,23 +43,23 @@ def tile_attend_colbert_proj_kernel(tc, emb_words, emb_scales, wp, qt, offs, out
         wp_raw = keep.tile([P, PACK, PROJ], F32, name="wp_raw")
         nc.sync.dma_start(wp_raw[:], wp_rows)
         nc.sync.dma_start(pool_words[:].bitcast(I32), emb_words[0].bitcast(I32))
+        qt_rows = qt.rearrange("(p j) q -> p j q", j=PACK)
+        qt_raw = [shared.tile([P, PACK, P], F32, name="qt_raw%d" % h, offset=4096 * (1 - h), align_bytes=64) for h in range(2)]
+        nc.sync.dma_start(qt_raw[0][:], qt_rows[:, :, 0:P])
         nc.vector.tensor_copy(slot_scales[:], pool_scales[:].indirect(offsets[:]))
         for r in range(4):
             nc.sync.dma_start(plane[r:P:32, :].bitcast(I32), slot_scales[112 + r : P : 4, :].bitcast(I32))
-        qt_raw = shared.tile([P, PACK, Q], F32, name="qt_raw", offset=0, align_bytes=64)
-        nc.sync.dma_start(qt_raw[:], qt.rearrange("(p j) q -> p j q", j=PACK))
+        nc.sync.dma_start(qt_raw[1][:], qt_rows[:, :, P : 2 * P])
 
         slot_words = {}
         wp_bf = shared.tile([P, PACK * P * PACK], BF16, name="wp_bf", offset=12288, align_bytes=64)
         wp_codes = keep.tile([P, PROJ], U32, name="wp_codes", align_bytes=64)
         wp_scales = keep.tile([P, PROJ], U8, name="wp_scales", align_bytes=64)
-        qt_bf = keep.tile([P, Q * PACK], BF16, name="qt_bf", align_bytes=64)
-        qt_codes = keep.tile([P, Q], U32, name="qt_codes", align_bytes=64)
         qt_scales = keep.tile([P, Q], U8, name="qt_scales", align_bytes=64)
         dt_bf = {}
         dt_codes = keep.tile([P, SLOTS], U32, name="dt_codes", align_bytes=64)
         dt_scales = keep.tile([P, SLOTS], U8, name="dt_scales", align_bytes=64)
-        out_rows = out.rearrange("(p h) g -> p h g", h=2)
+        out_rows = out.rearrange("(h p) g -> p h g", h=2)
         best = {}
 
         def copy_on(engine, dst, src):
@@ -82,10 +82,12 @@ def tile_attend_colbert_proj_kernel(tc, emb_words, emb_scales, wp, qt, offs, out
         def quantize(codes, scales, values, a, b):
             nc.vector.quantize_mx(out=codes[:, a:b].bitcast(FP8X4), scales=scales[:, a:b], in_=values[:, PACK * a : PACK * b])
 
-        def round_qt(engine, m0, m1):
-            dst = qt_bf[:].rearrange("p (h c u j) -> p c j u h", h=2, u=2, j=PACK)[:, m0:m1]
-            src = qt_raw[:].rearrange("p j (c u h) -> p c j u h", u=2, h=2)[:, m0:m1]
+        def round_qt(engine, h, place):
+            qt_bf = shared.tile([P, P * PACK], BF16, name="qt_bf%d" % h, offset=place, align_bytes=64)
+            dst = qt_bf[:].rearrange("p (c i j) -> p c j i", i=4, j=PACK)
+            src = qt_raw[h][:].rearrange("p j (c i) -> p c j i", i=4)
             copy_on(engine, dst, src)
+            return qt_bf
 
         banks = {}
 
@@ -144,17 +146,18 @@ def tile_attend_colbert_proj_kernel(tc, emb_words, emb_scales, wp, qt, offs, out
         def qd(a, b):
             nc.vector.quantize_mx(out=dt_codes[:, a:b].bitcast(FP8X4), scales=dt_scales[:, a:b], in_=dt_bf[a // CHUNK][:])
 
-        round_wp("scalar", 0, 32)
-        round_wp("vector", 32, 128)
-        quantize(wp_codes, wp_scales, wp_bf, 0, 512)
+        round_wp("scalar", 0, 36)
+        round_wp("vector", 36, 128)
+        quantize(wp_codes, wp_scales, wp_bf, 0, 256)
+        quantize(wp_codes, wp_scales, wp_bf, 256, 512)
         idle_bank = score_banks.tile([P, 2, 256], F32, name="score")
-        for i in range(3):
+        for n in (256, 512, 512):
             nc.tensor.matmul_mx(
-                out=idle_bank[:].rearrange("p h n -> p (h n)"),
+                out=idle_bank[:].rearrange("p h n -> p (h n)")[:, 0:n],
                 lhsT=wp_codes[:, 0:P].bitcast(FP8X4),
                 lhsT_scale=wp_scales[:, 0:P],
-                rhs=wp_codes[:].bitcast(FP8X4),
-                rhs_scale=wp_scales[:],
+                rhs=wp_codes[:, 0:n].bitcast(FP8X4),
+                rhs_scale=wp_scales[:, 0:n],
                 start=True,
                 stop=True,
             )
@@ -165,12 +168,14 @@ def tile_attend_colbert_proj_kernel(tc, emb_words, emb_scales, wp, qt, offs, out
         project(2)
         project(3)
         project(4)
+        qt_codes = keep.tile([P, Q], U32, name="qt_codes", align_bytes=64)
+        for h, engine, place in ((0, "scalar", 24576), (1, "vector", 25600)):
+            qt_bf = round_qt(engine, h, place)
+            nc.vector.quantize_mx(out=qt_codes[:, h * P : (h + 1) * P].bitcast(FP8X4), scales=qt_scales[:, h * P : (h + 1) * P], in_=qt_bf[:])
         round_dt("scalar", 0)
         project(5)
         round_dt("vector", 1)
         project(6)
-        round_qt("vector", 0, 64)
-        quantize(qt_codes, qt_scales, qt_bf, 0, 256)
         qd(0, 256)
         round_dt("scalar", 2)
         project(7)

@@ -18,7 +18,7 @@ P = 128
 PACK = 4
 CHUNK = 128
 RUN = 16
-STORES = ((0, 2, 6144), (2, 4, 8192), (4, 8, 11264),)
+STORES = ((0, 2, 26624), (2, 4, 26880), (4, 8, 27136),)
 GROUPS = ((0, 2, 4096), (2, 4, 6144), (4, 6, 8192), (6, 7, 10240), (7, 8, 11264))
 
 
@@ -82,12 +82,17 @@ def tile_attend_colbert_proj_kernel(tc, emb_words, emb_scales, wp, qt, offs, out
         def quantize(codes, scales, values, a, b):
             nc.vector.quantize_mx(out=codes[:, a:b].bitcast(FP8X4), scales=scales[:, a:b], in_=values[:, PACK * a : PACK * b])
 
-        def round_qt(engine, h, place):
-            qt_bf = shared.tile([P, P * PACK], BF16, name="qt_bf%d" % h, offset=place, align_bytes=64)
-            dst = qt_bf[:].rearrange("p (c i j) -> p c j i", i=4, j=PACK)
-            src = qt_raw[h][:].rearrange("p j (c i) -> p c j i", i=4)
+        qt_both = keep.tile([P, Q * PACK], BF16, name="qt_both", align_bytes=64)
+
+        def round_qt(engine, h):
+            qt_bf = qt_both[:, h * P * PACK : (h + 1) * P * PACK]
+            if engine == "gpsimd":
+                dst = qt_bf.rearrange("p (c j) -> p c j", j=PACK)
+                src = qt_raw[h][:].rearrange("p j c -> p c j")
+            else:
+                dst = qt_bf.rearrange("p (c i j) -> p c j i", i=4, j=PACK)
+                src = qt_raw[h][:].rearrange("p j (c i) -> p c j i", i=4)
             copy_on(engine, dst, src)
-            return qt_bf
 
         banks = {}
 
@@ -169,15 +174,15 @@ def tile_attend_colbert_proj_kernel(tc, emb_words, emb_scales, wp, qt, offs, out
         project(3)
         project(4)
         qt_codes = keep.tile([P, Q], U32, name="qt_codes", align_bytes=64)
-        for h, engine, place in ((0, "scalar", 24576), (1, "vector", 25600)):
-            qt_bf = round_qt(engine, h, place)
-            nc.vector.quantize_mx(out=qt_codes[:, h * P : (h + 1) * P].bitcast(FP8X4), scales=qt_scales[:, h * P : (h + 1) * P], in_=qt_bf[:])
+        round_qt("scalar", 0)
+        round_qt("gpsimd", 1)
         round_dt("scalar", 0)
         project(5)
-        round_dt("vector", 1)
+        round_dt("scalar", 1)
         project(6)
+        round_dt("vector", 2)
+        quantize(qt_codes, qt_scales, qt_both, 0, Q)
         qd(0, 256)
-        round_dt("scalar", 2)
         project(7)
         score(0, 256)
         round_dt("scalar", 3)

@@ -156,7 +156,7 @@ def tile_attend_colbert_proj_kernel(tc, emb_words, emb_scales, wp, qt, offs, out
         quantize(wp_codes, wp_scales, wp_bf, 0, 256)
         quantize(wp_codes, wp_scales, wp_bf, 256, 512)
         idle_bank = score_banks.tile([P, 2, 256], F32, name="score")
-        for n in (256, 512, 512):
+        for n in (256, 256, 512, 512):
             nc.tensor.matmul_mx(
                 out=idle_bank[:].rearrange("p h n -> p (h n)")[:, 0:n],
                 lhsT=wp_codes[:, 0:P].bitcast(FP8X4),

@@ -52,7 +52,7 @@ def tile_attend_colbert_proj_kernel(tc, emb_words, emb_scales, wp, qt, offs, out
         nc.sync.dma_start(qt_raw[1][:], qt_rows[:, :, P : 2 * P])
 
         slot_words = {}
-        wp_bf = shared.tile([P, PACK * P * PACK], BF16, name="wp_bf", offset=12288, align_bytes=64)
+        wp_bf = [shared.tile([P, 2 * P * PACK], BF16, name="wp_bf%d" % u, offset=12288 + 2048 * u, align_bytes=64) for u in range(2)]
         wp_codes = keep.tile([P, PROJ], U32, name="wp_codes", align_bytes=64)
         wp_scales = keep.tile([P, PROJ], U8, name="wp_scales", align_bytes=64)
         qt_scales = keep.tile([P, Q], U8, name="qt_scales", align_bytes=64)
@@ -71,12 +71,12 @@ def tile_attend_colbert_proj_kernel(tc, emb_words, emb_scales, wp, qt, offs, out
                 nc.vector.tensor_copy(dst, src)
 
         def gather_words(h):
-            slot_words[h] = shared.tile([P, SLOTS // 2], U16, name="slot_words%d" % h, offset=12288 + SLOTS * h, align_bytes=64)
+            slot_words[h] = shared.tile([P, SLOTS // 2], U16, name="slot_words%d" % h, offset=13824 + SLOTS * h, align_bytes=64)
             nc.vector.tensor_copy(slot_words[h][:], pool_words[:].indirect(offsets[:, 32 * h : 32 * (h + 1)]))
 
-        def round_wp(engine, m0, m1):
-            dst = wp_bf[:].rearrange("p (t m j) -> p m j t", t=PACK, j=PACK)[:, m0:m1]
-            src = wp_raw[:].rearrange("p j (m t) -> p m j t", t=PACK)[:, m0:m1]
+        def round_wp(engine, u, m0, m1):
+            dst = wp_bf[u][:].rearrange("p (t m j) -> p m j t", t=2, j=PACK)[:, m0:m1]
+            src = wp_raw[:].rearrange("p j (m t) -> p m j t", t=PACK)[:, m0:m1, :, 2 * u : 2 * u + 2]
             copy_on(engine, dst, src)
 
         def quantize(codes, scales, values, a, b):
@@ -151,10 +151,11 @@ def tile_attend_colbert_proj_kernel(tc, emb_words, emb_scales, wp, qt, offs, out
         def qd(a, b):
             nc.vector.quantize_mx(out=dt_codes[:, a:b].bitcast(FP8X4), scales=dt_scales[:, a:b], in_=dt_bf[a // CHUNK][:])
 
-        round_wp("scalar", 0, 36)
-        round_wp("vector", 36, 128)
-        quantize(wp_codes, wp_scales, wp_bf, 0, 256)
-        quantize(wp_codes, wp_scales, wp_bf, 256, 512)
+        for u, split in ((0, 40), (1, 76)):
+            round_wp("scalar", u, 0, split)
+            round_wp("vector", u, split, P)
+        for u in range(2):
+            nc.vector.quantize_mx(out=wp_codes[:, 256 * u : 256 * (u + 1)].bitcast(FP8X4), scales=wp_scales[:, 256 * u : 256 * (u + 1)], in_=wp_bf[u][:])
         idle_bank = score_banks.tile([P, 2, 256], F32, name="score")
         for n in (256, 256, 512, 512):
             nc.tensor.matmul_mx(

@@ -2,7 +2,7 @@ from contextlib import ExitStack
 
 import concourse.mybir as mybir
 
-K, T, SLOTS, PROJ, Q, G = 512, 4096, 1024, 512, 256, 64
+K, T, SLOTS, PROJ, Q = 512, 4096, 1024, 512, 256
 FLOPS = 2 * K * PROJ * SLOTS + 2 * PROJ * Q * SLOTS
 
 F32 = mybir.dt.float32
@@ -16,10 +16,29 @@ FP4X4 = mybir.dt.float4_e2m1fn_x4
 
 P = 128
 PACK = 4
-CHUNK = 128
 RUN = 16
-STORES = ((0, 2, 26624), (2, 4, 26880), (4, 8, 27136),)
-GROUPS = ((0, 2, 4096), (2, 4, 6144), (4, 6, 8192), (6, 7, 10240), (7, 8, 11264))
+LIST_ROWS = 16
+SCALE_ROWS = K // 32
+QUADRANT = 32
+HALF = SLOTS // 2
+CHUNK = 128
+CHUNKS = SLOTS // CHUNK
+PROJ_BANKS, SCORE_BANKS = 5, 3
+
+GROUPS = ((0, 2), (2, 4), (4, 6), (6, 7), (7, 8))
+STORES = ((0, 2), (2, 4), (4, 8))
+MAX_LAG = 2
+VECTOR_CHUNK = 2
+SCALAR_PLACES = (40, 76)
+WARM_UP = (256, 256, 512, 512)
+
+SCALE_POOL_AT = 0
+QT_RAW_BYTES = PACK * P * 4
+QT_RAW_AT = (T, SCALE_POOL_AT)
+FIRST_DT_AT = QT_RAW_AT[0]
+WP_BF_BYTES = 2 * P * PACK * 2
+WP_BF_AT = (T + QT_RAW_BYTES, T + QT_RAW_BYTES + WP_BF_BYTES)
+SLOT_WORDS_AT = (WP_BF_AT[1] - HALF, WP_BF_AT[1] + HALF)
 
 
 def tile_attend_colbert_proj_kernel(tc, emb_words, emb_scales, wp, qt, offs, out):
@@ -27,180 +46,160 @@ def tile_attend_colbert_proj_kernel(tc, emb_words, emb_scales, wp, qt, offs, out
     with ExitStack() as ctx:
         keep = ctx.enter_context(tc.tile_pool(name="keep", bufs=1))
         shared = ctx.enter_context(tc.tile_pool(name="shared", bufs=1))
-        proj_banks = ctx.enter_context(tc.psum_pool(name="proj_banks", bufs=5))
-        score_banks = ctx.enter_context(tc.psum_pool(name="score_banks", bufs=3))
+        proj_banks = ctx.enter_context(tc.psum_pool(name="proj_banks", bufs=PROJ_BANKS))
+        score_banks = ctx.enter_context(tc.psum_pool(name="score_banks", bufs=SCORE_BANKS))
 
-        offsets = keep.tile([P, SLOTS // 16], U16, name="offsets")
-        pool_words = shared.tile([P, T], U16, name="pool_words", offset=16384, align_bytes=64)
-        pool_scales = shared.tile([P, T], U8, name="pool_scales", offset=0, align_bytes=64)
-        slot_scales = keep.tile([P, SLOTS], U8, name="slot_scales", align_bytes=64)
-        plane = keep.tile([P, SLOTS], U8, name="plane", align_bytes=64)
-        nc.vector.memset(pool_scales[0:112, :].bitcast(I32), 0)
-        nc.vector.memset(plane[:].bitcast(I32), 0)
-        nc.sync.dma_start(offsets[:], offs)
-        nc.sync.dma_start(pool_scales[112:P, :].bitcast(I32), emb_scales[0].bitcast(I32))
-        wp_rows = wp.rearrange("(p j) c -> p j c", j=PACK)
+        offsets = keep.tile([P, SLOTS // LIST_ROWS], U16, name="offsets")
+        pool_scales = shared.tile([P, T], U8, name="pool_scales", offset=SCALE_POOL_AT, align_bytes=64)
+        emb_plane = keep.tile([P, SLOTS], U8, name="emb_plane", align_bytes=64)
+        first_row = P - SCALE_ROWS
+        nc.vector.memset(pool_scales[0:first_row, :].bitcast(I32), 0)
+        nc.vector.memset(emb_plane[:].bitcast(I32), 0)
+
         wp_raw = keep.tile([P, PACK, PROJ], F32, name="wp_raw")
-        nc.sync.dma_start(wp_raw[:], wp_rows)
-        nc.sync.dma_start(pool_words[:].bitcast(I32), emb_words[0].bitcast(I32))
+        pool_words = keep.tile([P, T], U16, name="pool_words", align_bytes=64)
+        qt_raw = [shared.tile([P, PACK, P], F32, name="qt_raw%d" % h, offset=QT_RAW_AT[h], align_bytes=64) for h in range(2)]
         qt_rows = qt.rearrange("(p j) q -> p j q", j=PACK)
-        qt_raw = [shared.tile([P, PACK, P], F32, name="qt_raw%d" % h, offset=4096 * (1 - h), align_bytes=64) for h in range(2)]
+        nc.sync.dma_start(offsets[:], offs)
+        nc.sync.dma_start(pool_scales[first_row:P, :].bitcast(I32), emb_scales[0].bitcast(I32))
+        nc.sync.dma_start(wp_raw[:], wp.rearrange("(p j) c -> p j c", j=PACK))
+        nc.sync.dma_start(pool_words[:].bitcast(I32), emb_words[0].bitcast(I32))
         nc.sync.dma_start(qt_raw[0][:], qt_rows[:, :, 0:P])
+
+        slot_scales = keep.tile([P, SLOTS], U8, name="slot_scales", align_bytes=64)
         nc.vector.tensor_copy(slot_scales[:], pool_scales[:].indirect(offsets[:]))
         for r in range(4):
-            nc.sync.dma_start(plane[r:P:32, :].bitcast(I32), slot_scales[112 + r : P : 4, :].bitcast(I32))
-        nc.sync.dma_start(qt_raw[1][:], qt_rows[:, :, P : 2 * P])
+            nc.sync.dma_start(emb_plane[r:P:QUADRANT, :].bitcast(I32), slot_scales[first_row + r : P : 4, :].bitcast(I32))
+        nc.sync.dma_start(qt_raw[1][:], qt_rows[:, :, P:Q])
 
-        slot_words = {}
-        wp_bf = [shared.tile([P, 2 * P * PACK], BF16, name="wp_bf%d" % u, offset=12288 + 2048 * u, align_bytes=64) for u in range(2)]
+        def quantize(codes, plane, first, last, values):
+            nc.vector.quantize_mx(out=codes[:, first:last].bitcast(FP8X4), scales=plane[:, first:last], in_=values)
+
+        def multiply(result, codes, plane, first, moving, moving_plane):
+            nc.tensor.matmul_mx(
+                out=result,
+                lhsT=codes[:, first : first + P].bitcast(FP8X4),
+                lhsT_scale=plane[:, first : first + P],
+                rhs=moving,
+                rhs_scale=moving_plane,
+                start=True,
+                stop=True,
+            )
+
+        wp_bf = [shared.tile([P, 2 * P * PACK], BF16, name="wp_bf%d" % u, offset=WP_BF_AT[u], align_bytes=64) for u in range(2)]
         wp_codes = keep.tile([P, PROJ], U32, name="wp_codes", align_bytes=64)
-        wp_scales = keep.tile([P, PROJ], U8, name="wp_scales", align_bytes=64)
-        qt_scales = keep.tile([P, Q], U8, name="qt_scales", align_bytes=64)
-        dt_bf = {}
-        dt_codes = keep.tile([P, SLOTS], U32, name="dt_codes", align_bytes=64)
-        dt_scales = keep.tile([P, SLOTS], U8, name="dt_scales", align_bytes=64)
-        out_rows = out.rearrange("(h p) g -> p h g", h=2)
-        best = {}
+        wp_plane = keep.tile([P, PROJ], U8, name="wp_plane", align_bytes=64)
+        for u, split in enumerate(SCALAR_PLACES):
+            dealt = wp_bf[u][:].rearrange("p (t m j) -> p m j t", t=2, j=PACK)
+            rows = wp_raw[:].rearrange("p j (m t) -> p m j t", t=PACK)[:, :, :, 2 * u : 2 * u + 2]
+            nc.scalar.copy(dealt[:, 0:split], rows[:, 0:split])
+            nc.vector.tensor_copy(dealt[:, split:P], rows[:, split:P])
+        for u in range(2):
+            quantize(wp_codes, wp_plane, 2 * P * u, 2 * P * (u + 1), wp_bf[u][:])
 
-        def copy_on(engine, dst, src):
-            if engine == "scalar":
-                nc.scalar.copy(dst, src)
-            elif engine == "gpsimd":
-                nc.gpsimd.tensor_scalar(dst, src, 1.0, 0.0, mybir.AluOpType.mult, mybir.AluOpType.add)
-            else:
-                nc.vector.tensor_copy(dst, src)
+        idle_bank = score_banks.tile([P, 2 * Q], F32, name="score")
+        for n in WARM_UP:
+            multiply(idle_bank[:, 0:n], wp_codes, wp_plane, 0, wp_codes[:, 0:n].bitcast(FP8X4), wp_plane[:, 0:n])
 
-        def gather_words(h):
-            slot_words[h] = shared.tile([P, SLOTS // 2], U16, name="slot_words%d" % h, offset=13824 + SLOTS * h, align_bytes=64)
-            nc.vector.tensor_copy(slot_words[h][:], pool_words[:].indirect(offsets[:, 32 * h : 32 * (h + 1)]))
-
-        def round_wp(engine, u, m0, m1):
-            dst = wp_bf[u][:].rearrange("p (t m j) -> p m j t", t=2, j=PACK)[:, m0:m1]
-            src = wp_raw[:].rearrange("p j (m t) -> p m j t", t=PACK)[:, m0:m1, :, 2 * u : 2 * u + 2]
-            copy_on(engine, dst, src)
-
-        def quantize(codes, scales, values, a, b):
-            nc.vector.quantize_mx(out=codes[:, a:b].bitcast(FP8X4), scales=scales[:, a:b], in_=values[:, PACK * a : PACK * b])
-
-        qt_both = keep.tile([P, Q * PACK], BF16, name="qt_both", align_bytes=64)
-
-        def round_qt(engine, h):
-            qt_bf = qt_both[:, h * P * PACK : (h + 1) * P * PACK]
-            if engine == "gpsimd":
-                dst = qt_bf.rearrange("p (c j) -> p c j", j=PACK)
-                src = qt_raw[h][:].rearrange("p j c -> p c j")
-            else:
-                dst = qt_bf.rearrange("p (c i j) -> p c j i", i=4, j=PACK)
-                src = qt_raw[h][:].rearrange("p j (c i) -> p c j i", i=4)
-            copy_on(engine, dst, src)
+        slot_words = []
+        for h in range(2):
+            words = shared.tile([P, HALF], U16, name="slot_words%d" % h, offset=SLOT_WORDS_AT[h], align_bytes=64)
+            columns = HALF // LIST_ROWS
+            nc.vector.tensor_copy(words[:], pool_words[:].indirect(offsets[:, columns * h : columns * (h + 1)]))
+            slot_words.append(words)
 
         banks = {}
 
         def project(c):
-            bank = proj_banks.tile([P, PACK, CHUNK], F32, name="bank")
-            banks[c] = bank
-            h, lo = divmod(c * CHUNK, SLOTS // 2)
+            banks[c] = proj_banks.tile([P, PACK, CHUNK], F32, name="bank")
+            h, lo = divmod(c * CHUNK, HALF)
             for t in range(PACK):
-                nc.tensor.matmul_mx(
-                    out=bank[:, t, :],
-                    lhsT=wp_codes[:, t * P : (t + 1) * P].bitcast(FP8X4),
-                    lhsT_scale=wp_scales[:, t * P : (t + 1) * P],
-                    rhs=slot_words[h][:, lo : lo + CHUNK].bitcast(FP4X4),
-                    rhs_scale=plane[:, c * CHUNK : (c + 1) * CHUNK],
-                    start=True,
-                    stop=True,
+                multiply(
+                    banks[c][:, t, :],
+                    wp_codes,
+                    wp_plane,
+                    t * P,
+                    slot_words[h][:, lo : lo + CHUNK].bitcast(FP4X4),
+                    emb_plane[:, c * CHUNK : (c + 1) * CHUNK],
                 )
 
-        def round_dt(engine, c):
-            first, last, place = [g for g in GROUPS if g[0] <= c < g[1]][0]
-            if first not in dt_bf:
-                dt_bf[first] = shared.tile([P, (last - first) * CHUNK * PACK], BF16, name="dt_bf%d" % first, offset=place, align_bytes=64)
-            dst = dt_bf[first][:, (c - first) * CHUNK * PACK : (c - first + 1) * CHUNK * PACK].rearrange("p (n t) -> p n t", t=PACK)
-            copy_on(engine, dst, banks[c][:].rearrange("p t n -> p n t"))
+        for c in [0, VECTOR_CHUNK] + [c for c in range(1, PROJ_BANKS) if c != VECTOR_CHUNK]:
+            project(c)
 
+        qt_bf = keep.tile([P, 2, P * PACK], BF16, name="qt_bf", align_bytes=64)
+        nc.scalar.copy(
+            qt_bf[:, 0, :].rearrange("p (c i j) -> p c j i", i=4, j=PACK),
+            qt_raw[0][:].rearrange("p j (c i) -> p c j i", i=4),
+        )
+        nc.gpsimd.tensor_scalar(
+            qt_bf[:, 1, :].rearrange("p (c j) -> p c j", j=PACK),
+            qt_raw[1][:].rearrange("p j c -> p c j"),
+            1.0,
+            0.0,
+            mybir.AluOpType.mult,
+            mybir.AluOpType.add,
+        )
+
+        dt_bf = {}
+        for first, last in GROUPS:
+            shape = [P, (last - first) * CHUNK * PACK]
+            if first == 0:
+                dt_bf[first] = shared.tile(shape, BF16, name="dt_bf0", offset=FIRST_DT_AT, align_bytes=64)
+            else:
+                dt_bf[first] = keep.tile(shape, BF16, name="dt_bf%d" % first, align_bytes=64)
+
+        def empty_bank(c):
+            first = max(g for g in dt_bf if g <= c)
+            width = CHUNK * PACK
+            rounded = dt_bf[first][:, (c - first) * width : (c - first + 1) * width].rearrange("p (n t) -> p n t", t=PACK)
+            sums = banks[c][:].rearrange("p t n -> p n t")
+            if c == VECTOR_CHUNK:
+                nc.vector.tensor_copy(rounded, sums)
+            else:
+                nc.scalar.copy(rounded, sums)
+            if c + PROJ_BANKS < CHUNKS:
+                project(c + PROJ_BANKS)
+
+        qt_codes = keep.tile([P, Q], U32, name="qt_codes", align_bytes=64)
+        qt_plane = keep.tile([P, Q], U8, name="qt_plane", align_bytes=64)
+        dt_codes = keep.tile([P, SLOTS], U32, name="dt_codes", align_bytes=64)
+        dt_plane = keep.tile([P, SLOTS], U8, name="dt_plane", align_bytes=64)
         scores = {}
 
-        def score(a, b):
-            bank = score_banks.tile([P, 2, b - a], F32, name="score")
-            scores[a] = bank
+        def score(first, last):
+            a, b = first * CHUNK, last * CHUNK
+            scores[first] = score_banks.tile([P, 2, b - a], F32, name="score")
             for h in range(2):
-                nc.tensor.matmul_mx(
-                    out=bank[:, h, :],
-                    lhsT=qt_codes[:, h * P : (h + 1) * P].bitcast(FP8X4),
-                    lhsT_scale=qt_scales[:, h * P : (h + 1) * P],
-                    rhs=dt_codes[:, a:b].bitcast(FP8X4),
-                    rhs_scale=dt_scales[:, a:b],
-                    start=True,
-                    stop=True,
-                )
+                multiply(scores[first][:, h, :], qt_codes, qt_plane, h * P, dt_codes[:, a:b].bitcast(FP8X4), dt_plane[:, a:b])
 
-        def keep_best(a, b):
-            first, last, place = [g for g in STORES if g[0] * CHUNK <= a < g[1] * CHUNK][0]
-            g0, g1 = first * CHUNK // RUN, last * CHUNK // RUN
-            if first not in best:
-                best[first] = shared.tile([P, 2, g1 - g0], F32, name="best%d" % first, offset=place, align_bytes=64)
+        passages = CHUNK // RUN
+        out_rows = out.rearrange("(h p) g -> p h g", h=2)
+        best = {lo: keep.tile([P, 2, (hi - lo) * passages], F32, name="best%d" % lo, align_bytes=64) for lo, hi in STORES}
+
+        def keep_best(first, last):
+            lo, hi = [s for s in STORES if s[0] <= first < s[1]][0]
             nc.vector.tensor_reduce(
-                best[first][:, :, a // RUN - g0 : b // RUN - g0],
-                scores[a][:].rearrange("p h (g s) -> p h g s", s=RUN),
+                best[lo][:, :, (first - lo) * passages : (last - lo) * passages],
+                scores[first][:].rearrange("p h (g s) -> p h g s", s=RUN),
                 mybir.AxisListType.X,
                 mybir.AluOpType.max,
             )
-            if b == last * CHUNK:
-                nc.sync.dma_start(out_rows[:, :, g0:g1], best[first][:])
+            if last == hi:
+                nc.sync.dma_start(out_rows[:, :, lo * passages : hi * passages], best[lo][:])
 
-        def qd(a, b):
-            nc.vector.quantize_mx(out=dt_codes[:, a:b].bitcast(FP8X4), scales=dt_scales[:, a:b], in_=dt_bf[a // CHUNK][:])
+        for c in range(VECTOR_CHUNK + 1):
+            empty_bank(c)
+        quantize(qt_codes, qt_plane, 0, Q, qt_bf[:].rearrange("p h x -> p (h x)"))
 
-        for u, split in ((0, 40), (1, 76)):
-            round_wp("scalar", u, 0, split)
-            round_wp("vector", u, split, P)
-        for u in range(2):
-            nc.vector.quantize_mx(out=wp_codes[:, 256 * u : 256 * (u + 1)].bitcast(FP8X4), scales=wp_scales[:, 256 * u : 256 * (u + 1)], in_=wp_bf[u][:])
-        idle_bank = score_banks.tile([P, 2, 256], F32, name="score")
-        for n in (256, 256, 512, 512):
-            nc.tensor.matmul_mx(
-                out=idle_bank[:].rearrange("p h n -> p (h n)")[:, 0:n],
-                lhsT=wp_codes[:, 0:P].bitcast(FP8X4),
-                lhsT_scale=wp_scales[:, 0:P],
-                rhs=wp_codes[:, 0:n].bitcast(FP8X4),
-                rhs_scale=wp_scales[:, 0:n],
-                start=True,
-                stop=True,
-            )
-        gather_words(0)
-        gather_words(1)
-        project(0)
-        project(1)
-        project(2)
-        project(3)
-        project(4)
-        qt_codes = keep.tile([P, Q], U32, name="qt_codes", align_bytes=64)
-        round_qt("scalar", 0)
-        round_qt("gpsimd", 1)
-        round_dt("scalar", 0)
-        project(5)
-        round_dt("scalar", 1)
-        project(6)
-        round_dt("vector", 2)
-        quantize(qt_codes, qt_scales, qt_both, 0, Q)
-        qd(0, 256)
-        project(7)
-        score(0, 256)
-        round_dt("scalar", 3)
-        qd(256, 512)
-        keep_best(0, 256)
-        score(256, 512)
-        round_dt("scalar", 4)
-        round_dt("scalar", 5)
-        qd(512, 768)
-        keep_best(256, 512)
-        score(512, 768)
-        round_dt("scalar", 6)
-        qd(768, 896)
-        score(768, 896)
-        round_dt("scalar", 7)
-        qd(896, 1024)
-        keep_best(512, 768)
-        score(896, 1024)
-        keep_best(768, 896)
-        keep_best(896, 1024)
+        waiting = []
+        for first, last in GROUPS:
+            for c in range(max(first, VECTOR_CHUNK + 1), last):
+                empty_bank(c)
+            quantize(dt_codes, dt_plane, first * CHUNK, last * CHUNK, dt_bf[first][:])
+            for group in [g for g in waiting if g[1] + MAX_LAG <= last]:
+                keep_best(*group)
+                waiting.remove(group)
+            score(first, last)
+            waiting.append((first, last))
+        for group in waiting:
+            keep_best(*group)

@@ -30,7 +30,6 @@ STORES = ((0, 2), (2, 4), (4, 8))
 MAX_LAG = 2
 VECTOR_CHUNK = 2
 SCALAR_PLACES = (40, 76)
-WARM_UP = (256, 256, 512, 512)
 
 SCALE_POOL_AT = 0
 QT_RAW_BYTES = PACK * P * 4
@@ -96,10 +95,6 @@ def tile_attend_colbert_proj_kernel(tc, emb_words, emb_scales, wp, qt, offs, out
             nc.vector.tensor_copy(dealt[:, split:P], rows[:, split:P])
         for u in range(2):
             quantize(wp_codes, wp_plane, 2 * P * u, 2 * P * (u + 1), wp_bf[u][:])
-
-        idle_bank = score_banks.tile([P, 2 * Q], F32, name="score")
-        for n in WARM_UP:
-            multiply(idle_bank[:, 0:n], wp_codes, wp_plane, 0, wp_codes[:, 0:n].bitcast(FP8X4), wp_plane[:, 0:n])
 
         slot_words = []
         for h in range(2):

@@ -30,6 +30,7 @@ STORES = ((0, 2), (2, 4), (4, 8))
 MAX_LAG = 2
 VECTOR_CHUNK = 2
 SCALAR_PLACES = (40, 76)
+SCALAR_QUERIES = 64
 
 SCALE_POOL_AT = 0
 QT_RAW_BYTES = PACK * P * 4
@@ -38,6 +39,7 @@ FIRST_DT_AT = QT_RAW_AT[0]
 WP_BF_BYTES = 2 * P * PACK * 2
 WP_BF_AT = (T + QT_RAW_BYTES, T + QT_RAW_BYTES + WP_BF_BYTES)
 SLOT_WORDS_AT = (WP_BF_AT[1] - HALF, WP_BF_AT[1] + HALF)
+QT_BF_AT = WP_BF_AT[1] + WP_BF_BYTES
 
 
 def tile_attend_colbert_proj_kernel(tc, emb_words, emb_scales, wp, qt, offs, out):
@@ -57,19 +59,22 @@ def tile_attend_colbert_proj_kernel(tc, emb_words, emb_scales, wp, qt, offs, out
 
         wp_raw = keep.tile([P, PACK, PROJ], F32, name="wp_raw")
         pool_words = keep.tile([P, T], U16, name="pool_words", align_bytes=64)
-        qt_raw = [shared.tile([P, PACK, P], F32, name="qt_raw%d" % h, offset=QT_RAW_AT[h], align_bytes=64) for h in range(2)]
+        qt_raw = [
+            shared.tile([P, PACK, n], F32, name="qt_raw%d" % h, offset=QT_RAW_AT[h], align_bytes=64)
+            for h, n in enumerate((SCALAR_QUERIES, Q - SCALAR_QUERIES))
+        ]
         qt_rows = qt.rearrange("(p j) q -> p j q", j=PACK)
         nc.sync.dma_start(offsets[:], offs)
         nc.sync.dma_start(pool_scales[first_row:P, :].bitcast(I32), emb_scales[0].bitcast(I32))
         nc.sync.dma_start(wp_raw[:], wp.rearrange("(p j) c -> p j c", j=PACK))
         nc.sync.dma_start(pool_words[:].bitcast(I32), emb_words[0].bitcast(I32))
-        nc.sync.dma_start(qt_raw[0][:], qt_rows[:, :, 0:P])
+        nc.sync.dma_start(qt_raw[0][:], qt_rows[:, :, 0:SCALAR_QUERIES])
 
         slot_scales = keep.tile([P, SLOTS], U8, name="slot_scales", align_bytes=64)
         nc.vector.tensor_copy(slot_scales[:], pool_scales[:].indirect(offsets[:]))
         for r in range(4):
             nc.sync.dma_start(emb_plane[r:P:QUADRANT, :].bitcast(I32), slot_scales[first_row + r : P : 4, :].bitcast(I32))
-        nc.sync.dma_start(qt_raw[1][:], qt_rows[:, :, P:Q])
+        nc.sync.dma_start(qt_raw[1][:], qt_rows[:, :, SCALAR_QUERIES:Q])
 
         def quantize(codes, plane, first, last, values):
             nc.vector.quantize_mx(out=codes[:, first:last].bitcast(FP8X4), scales=plane[:, first:last], in_=values)
@@ -121,13 +126,13 @@ def tile_attend_colbert_proj_kernel(tc, emb_words, emb_scales, wp, qt, offs, out
         for c in [0, VECTOR_CHUNK] + [c for c in range(1, PROJ_BANKS) if c != VECTOR_CHUNK]:
             project(c)
 
-        qt_bf = keep.tile([P, 2, P * PACK], BF16, name="qt_bf", align_bytes=64)
+        qt_bf = shared.tile([P, Q * PACK], BF16, name="qt_bf", offset=QT_BF_AT, align_bytes=64)
         nc.scalar.copy(
-            qt_bf[:, 0, :].rearrange("p (c i j) -> p c j i", i=4, j=PACK),
+            qt_bf[:, 0 : SCALAR_QUERIES * PACK].rearrange("p (c i j) -> p c j i", i=4, j=PACK),
             qt_raw[0][:].rearrange("p j (c i) -> p c j i", i=4),
         )
         nc.gpsimd.tensor_scalar(
-            qt_bf[:, 1, :].rearrange("p (c j) -> p c j", j=PACK),
+            qt_bf[:, SCALAR_QUERIES * PACK :].rearrange("p (c j) -> p c j", j=PACK),
             qt_raw[1][:].rearrange("p j c -> p c j"),
             1.0,
             0.0,
@@ -157,7 +162,7 @@ def tile_attend_colbert_proj_kernel(tc, emb_words, emb_scales, wp, qt, offs, out
 
         qt_codes = keep.tile([P, Q], U32, name="qt_codes", align_bytes=64)
         qt_plane = keep.tile([P, Q], U8, name="qt_plane", align_bytes=64)
-        dt_codes = keep.tile([P, SLOTS], U32, name="dt_codes", align_bytes=64)
+        dt_codes = shared.tile([P, SLOTS], U32, name="dt_codes", offset=QT_BF_AT, align_bytes=64)
         dt_plane = keep.tile([P, SLOTS], U8, name="dt_plane", align_bytes=64)
         scores = {}
 
@@ -184,7 +189,7 @@ def tile_attend_colbert_proj_kernel(tc, emb_words, emb_scales, wp, qt, offs, out
 
         for c in range(VECTOR_CHUNK + 1):
             empty_bank(c)
-        quantize(qt_codes, qt_plane, 0, Q, qt_bf[:].rearrange("p h x -> p (h x)"))
+        quantize(qt_codes, qt_plane, 0, Q, qt_bf[:])
 
         waiting = []
         for first, last in GROUPS:

@@ -31,6 +31,8 @@ MAX_LAG = 2
 VECTOR_CHUNK = 2
 SCALAR_PLACES = (40, 76)
 SCALAR_QUERIES = 64
+WARM_ROWS = 32
+WARM_WIDTHS = (128, 128, 512, 512, 512)
 
 SCALE_POOL_AT = 0
 QT_RAW_BYTES = PACK * P * 4
@@ -100,6 +102,18 @@ def tile_attend_colbert_proj_kernel(tc, emb_words, emb_scales, wp, qt, offs, out
             nc.vector.tensor_copy(dealt[:, split:P], rows[:, split:P])
         for u in range(2):
             quantize(wp_codes, wp_plane, 2 * P * u, 2 * P * (u + 1), wp_bf[u][:])
+
+        warm = score_banks.tile([WARM_ROWS, PROJ], F32, name="score")
+        for width in WARM_WIDTHS:
+            nc.tensor.matmul_mx(
+                out=warm[:, 0:width],
+                lhsT=wp_codes[:, 0:WARM_ROWS].bitcast(FP8X4),
+                lhsT_scale=wp_plane[:, 0:WARM_ROWS],
+                rhs=wp_codes[:, 0:width].bitcast(FP8X4),
+                rhs_scale=wp_plane[:, 0:width],
+                start=True,
+                stop=True,
+            )
 
         slot_words = []
         for h in range(2):

@@ -32,7 +32,7 @@ VECTOR_CHUNK = 2
 SCALAR_PLACES = (40, 76)
 SCALAR_QUERIES = 64
 WARM_ROWS = 32
-WARM_WIDTHS = (128, 128, 512, 512, 512)
+WARM_WIDTHS = (128, 128, 128, 128, 512, 512)
 
 SCALE_POOL_AT = 0
 QT_RAW_BYTES = PACK * P * 4

@@ -30,7 +30,7 @@ STORES = ((0, 2), (2, 4), (4, 8))
 MAX_LAG = 2
 VECTOR_CHUNK = 2
 SCALAR_PLACES = (40, 76)
-SCALAR_QUERIES = 64
+SCALAR_QUERIES = 128
 WARM_ROWS = 32
 WARM_WIDTHS = (128, 128, 128, 128, 512, 512)
 

@@ -28,7 +28,8 @@ PROJ_BANKS, SCORE_BANKS = 5, 3
 GROUPS = ((0, 2), (2, 4), (4, 6), (6, 7), (7, 8))
 STORES = ((0, 2), (2, 4), (4, 8))
 MAX_LAG = 2
-VECTOR_CHUNK = 2
+VECTOR_CHUNK = 1
+SHARED_CHUNK, VECTOR_SLOTS = 3, 48
 SCALAR_PLACES = (40, 76)
 SCALAR_QUERIES = 128
 WARM_ROWS = 32
@@ -137,7 +138,7 @@ def tile_attend_colbert_proj_kernel(tc, emb_words, emb_scales, wp, qt, offs, out
                     emb_plane[:, c * CHUNK : (c + 1) * CHUNK],
                 )
 
-        for c in [0, VECTOR_CHUNK] + [c for c in range(1, PROJ_BANKS) if c != VECTOR_CHUNK]:
+        for c in range(PROJ_BANKS):
             project(c)
 
         qt_bf = shared.tile([P, Q * PACK], BF16, name="qt_bf", offset=QT_BF_AT, align_bytes=64)
@@ -169,6 +170,9 @@ def tile_attend_colbert_proj_kernel(tc, emb_words, emb_scales, wp, qt, offs, out
             sums = banks[c][:].rearrange("p t n -> p n t")
             if c == VECTOR_CHUNK:
                 nc.vector.tensor_copy(rounded, sums)
+            elif c == SHARED_CHUNK:
+                nc.vector.tensor_copy(rounded[:, 0:VECTOR_SLOTS], sums[:, 0:VECTOR_SLOTS])
+                nc.scalar.copy(rounded[:, VECTOR_SLOTS:], sums[:, VECTOR_SLOTS:])
             else:
                 nc.scalar.copy(rounded, sums)
             if c + PROJ_BANKS < CHUNKS:
@@ -176,7 +180,7 @@ def tile_attend_colbert_proj_kernel(tc, emb_words, emb_scales, wp, qt, offs, out
 
         qt_codes = keep.tile([P, Q], U32, name="qt_codes", align_bytes=64)
         qt_plane = keep.tile([P, Q], U8, name="qt_plane", align_bytes=64)
-        dt_codes = shared.tile([P, SLOTS], U32, name="dt_codes", offset=QT_BF_AT, align_bytes=64)
+        dt_codes = keep.tile([P, SLOTS], U32, name="dt_codes", align_bytes=64)
         dt_plane = keep.tile([P, SLOTS], U8, name="dt_plane", align_bytes=64)
         scores = {}
 
@@ -201,15 +205,19 @@ def tile_attend_colbert_proj_kernel(tc, emb_words, emb_scales, wp, qt, offs, out
             if last == hi:
                 nc.sync.dma_start(out_rows[:, :, lo * passages : hi * passages], best[lo][:])
 
-        for c in range(VECTOR_CHUNK + 1):
+        quantize(qt_codes, qt_plane, 0, P, qt_bf[:, 0 : P * PACK])
+        for c in range(SHARED_CHUNK + 1):
             empty_bank(c)
-        quantize(qt_codes, qt_plane, 0, Q, qt_bf[:])
 
         waiting = []
         for first, last in GROUPS:
-            for c in range(max(first, VECTOR_CHUNK + 1), last):
+            for c in range(max(first, SHARED_CHUNK + 1), last):
                 empty_bank(c)
-            quantize(dt_codes, dt_plane, first * CHUNK, last * CHUNK, dt_bf[first][:])
+            cuts = range(first, last + 1) if first > SHARED_CHUNK else (first, last)
+            for a, b in zip(cuts, cuts[1:]):
+                quantize(dt_codes, dt_plane, a * CHUNK, b * CHUNK, dt_bf[first][:, (a - first) * CHUNK * PACK : (b - first) * CHUNK * PACK])
+            if first == 0:
+                quantize(qt_codes, qt_plane, P, Q, qt_bf[:, P * PACK :])
             for group in [g for g in waiting if g[1] + MAX_LAG <= last]:
                 keep_best(*group)
                 waiting.remove(group)

@@ -30,7 +30,7 @@ STORES = ((0, 2), (2, 4), (4, 8))
 MAX_LAG = 2
 VECTOR_CHUNK = 1
 SHARED_CHUNK, VECTOR_SLOTS = 3, 48
-SCALAR_PLACES = (40, 76)
+SCALAR_PLACES = (44, 84)
 SCALAR_QUERIES = 128
 WARM_ROWS = 32
 WARM_WIDTHS = (128, 128, 128, 128, 512, 512)
@@ -41,8 +41,9 @@ QT_RAW_AT = (T, SCALE_POOL_AT)
 FIRST_DT_AT = QT_RAW_AT[0]
 WP_BF_BYTES = 2 * P * PACK * 2
 WP_BF_AT = (T + QT_RAW_BYTES, T + QT_RAW_BYTES + WP_BF_BYTES)
-SLOT_WORDS_AT = (WP_BF_AT[1] - HALF, WP_BF_AT[1] + HALF)
 QT_BF_AT = WP_BF_AT[1] + WP_BF_BYTES
+WP_RAW_AT = QT_BF_AT + 2 * PACK * Q
+SLOT_WORDS_AT = (WP_RAW_AT, WP_RAW_AT + 2 * HALF)
 
 
 def tile_attend_colbert_proj_kernel(tc, emb_words, emb_scales, wp, qt, offs, out):
@@ -60,7 +61,7 @@ def tile_attend_colbert_proj_kernel(tc, emb_words, emb_scales, wp, qt, offs, out
         nc.vector.memset(pool_scales[0:first_row, :].bitcast(I32), 0)
         nc.vector.memset(emb_plane[:].bitcast(I32), 0)
 
-        wp_raw = keep.tile([P, PACK, PROJ], F32, name="wp_raw")
+        wp_raw = shared.tile([P, PACK, PROJ], F32, name="wp_raw", offset=WP_RAW_AT, align_bytes=64)
         pool_words = keep.tile([P, T], U16, name="pool_words", align_bytes=64)
         qt_raw = [
             shared.tile([P, PACK, n], F32, name="qt_raw%d" % h, offset=QT_RAW_AT[h], align_bytes=64)

@@ -30,7 +30,7 @@ STORES = ((0, 2), (2, 4), (4, 8))
 MAX_LAG = 2
 VECTOR_CHUNK = 1
 SHARED_CHUNK, VECTOR_SLOTS = 3, 48
-SCALAR_PLACES = (44, 84)
+SCALAR_PLACES = (40, 76)
 SCALAR_QUERIES = 128
 WARM_ROWS = 32
 WARM_WIDTHS = (128, 128, 128, 128, 512, 512)

from contextlib import ExitStack

import concourse.mybir as mybir

K, T, SLOTS, PROJ, Q = 512, 4096, 1024, 512, 256
FLOPS = 2 * K * PROJ * SLOTS + 2 * PROJ * Q * SLOTS

F32 = mybir.dt.float32
BF16 = mybir.dt.bfloat16
I32 = mybir.dt.int32
U32 = mybir.dt.uint32
U16 = mybir.dt.uint16
U8 = mybir.dt.uint8
FP8X4 = mybir.dt.float8_e4m3fn_x4
FP4X4 = mybir.dt.float4_e2m1fn_x4

P = 128
PACK = 4
RUN = 16
LIST_ROWS = 16
SCALE_ROWS = K // 32
QUADRANT = 32
HALF = SLOTS // 2
CHUNK = 128
CHUNKS = SLOTS // CHUNK
PROJ_BANKS, SCORE_BANKS = 5, 3

GROUPS = ((0, 2), (2, 4), (4, 6), (6, 7), (7, 8))
STORES = ((0, 2), (2, 4), (4, 8))
MAX_LAG = 2
VECTOR_CHUNK = 1
SHARED_CHUNK, VECTOR_SLOTS = 3, 48
SCALAR_PLACES = (40, 76)
SCALAR_QUERIES = 128
WARM_ROWS = 32
WARM_WIDTHS = (128, 128, 128, 128, 512, 512)

SCALE_POOL_AT = 0
QT_RAW_BYTES = PACK * P * 4
QT_RAW_AT = (T, SCALE_POOL_AT)
FIRST_DT_AT = QT_RAW_AT[0]
WP_BF_BYTES = 2 * P * PACK * 2
WP_BF_AT = (T + QT_RAW_BYTES, T + QT_RAW_BYTES + WP_BF_BYTES)
QT_BF_AT = WP_BF_AT[1] + WP_BF_BYTES
WP_RAW_AT = QT_BF_AT + 2 * PACK * Q
SLOT_WORDS_AT = (WP_RAW_AT, WP_RAW_AT + 2 * HALF)


def tile_attend_colbert_proj_kernel(tc, emb_words, emb_scales, wp, qt, offs, out):
    nc = tc.nc
    with ExitStack() as ctx:
        keep = ctx.enter_context(tc.tile_pool(name="keep", bufs=1))
        shared = ctx.enter_context(tc.tile_pool(name="shared", bufs=1))
        proj_banks = ctx.enter_context(tc.psum_pool(name="proj_banks", bufs=PROJ_BANKS))
        score_banks = ctx.enter_context(tc.psum_pool(name="score_banks", bufs=SCORE_BANKS))

        offsets = keep.tile([P, SLOTS // LIST_ROWS], U16, name="offsets")
        pool_scales = shared.tile([P, T], U8, name="pool_scales", offset=SCALE_POOL_AT, align_bytes=64)
        emb_plane = keep.tile([P, SLOTS], U8, name="emb_plane", align_bytes=64)
        first_row = P - SCALE_ROWS
        nc.vector.memset(pool_scales[0:first_row, :].bitcast(I32), 0)
        nc.vector.memset(emb_plane[:].bitcast(I32), 0)

        wp_raw = shared.tile([P, PACK, PROJ], F32, name="wp_raw", offset=WP_RAW_AT, align_bytes=64)
        pool_words = keep.tile([P, T], U16, name="pool_words", align_bytes=64)
        qt_raw = [
            shared.tile([P, PACK, n], F32, name="qt_raw%d" % h, offset=QT_RAW_AT[h], align_bytes=64)
            for h, n in enumerate((SCALAR_QUERIES, Q - SCALAR_QUERIES))
        ]
        qt_rows = qt.rearrange("(p j) q -> p j q", j=PACK)
        nc.sync.dma_start(offsets[:], offs)
        nc.sync.dma_start(pool_scales[first_row:P, :].bitcast(I32), emb_scales[0].bitcast(I32))
        nc.sync.dma_start(wp_raw[:], wp.rearrange("(p j) c -> p j c", j=PACK))
        nc.sync.dma_start(pool_words[:].bitcast(I32), emb_words[0].bitcast(I32))
        nc.sync.dma_start(qt_raw[0][:], qt_rows[:, :, 0:SCALAR_QUERIES])

        slot_scales = keep.tile([P, SLOTS], U8, name="slot_scales", align_bytes=64)
        nc.vector.tensor_copy(slot_scales[:], pool_scales[:].indirect(offsets[:]))
        for r in range(4):
            nc.sync.dma_start(emb_plane[r:P:QUADRANT, :].bitcast(I32), slot_scales[first_row + r : P : 4, :].bitcast(I32))
        nc.sync.dma_start(qt_raw[1][:], qt_rows[:, :, SCALAR_QUERIES:Q])

        def quantize(codes, plane, first, last, values):
            nc.vector.quantize_mx(out=codes[:, first:last].bitcast(FP8X4), scales=plane[:, first:last], in_=values)

        def multiply(result, codes, plane, first, moving, moving_plane):
            nc.tensor.matmul_mx(
                out=result,
                lhsT=codes[:, first : first + P].bitcast(FP8X4),
                lhsT_scale=plane[:, first : first + P],
                rhs=moving,
                rhs_scale=moving_plane,
                start=True,
                stop=True,
            )

        wp_bf = [shared.tile([P, 2 * P * PACK], BF16, name="wp_bf%d" % u, offset=WP_BF_AT[u], align_bytes=64) for u in range(2)]
        wp_codes = keep.tile([P, PROJ], U32, name="wp_codes", align_bytes=64)
        wp_plane = keep.tile([P, PROJ], U8, name="wp_plane", align_bytes=64)
        for u, split in enumerate(SCALAR_PLACES):
            dealt = wp_bf[u][:].rearrange("p (t m j) -> p m j t", t=2, j=PACK)
            rows = wp_raw[:].rearrange("p j (m t) -> p m j t", t=PACK)[:, :, :, 2 * u : 2 * u + 2]
            nc.scalar.copy(dealt[:, 0:split], rows[:, 0:split])
            nc.vector.tensor_copy(dealt[:, split:P], rows[:, split:P])
        for u in range(2):
            quantize(wp_codes, wp_plane, 2 * P * u, 2 * P * (u + 1), wp_bf[u][:])

        warm = score_banks.tile([WARM_ROWS, PROJ], F32, name="score")
        for width in WARM_WIDTHS:
            nc.tensor.matmul_mx(
                out=warm[:, 0:width],
                lhsT=wp_codes[:, 0:WARM_ROWS].bitcast(FP8X4),
                lhsT_scale=wp_plane[:, 0:WARM_ROWS],
                rhs=wp_codes[:, 0:width].bitcast(FP8X4),
                rhs_scale=wp_plane[:, 0:width],
                start=True,
                stop=True,
            )

        slot_words = []
        for h in range(2):
            words = shared.tile([P, HALF], U16, name="slot_words%d" % h, offset=SLOT_WORDS_AT[h], align_bytes=64)
            columns = HALF // LIST_ROWS
            nc.vector.tensor_copy(words[:], pool_words[:].indirect(offsets[:, columns * h : columns * (h + 1)]))
            slot_words.append(words)

        banks = {}

        def project(c):
            banks[c] = proj_banks.tile([P, PACK, CHUNK], F32, name="bank")
            h, lo = divmod(c * CHUNK, HALF)
            for t in range(PACK):
                multiply(
                    banks[c][:, t, :],
                    wp_codes,
                    wp_plane,
                    t * P,
                    slot_words[h][:, lo : lo + CHUNK].bitcast(FP4X4),
                    emb_plane[:, c * CHUNK : (c + 1) * CHUNK],
                )

        for c in range(PROJ_BANKS):
            project(c)

        qt_bf = shared.tile([P, Q * PACK], BF16, name="qt_bf", offset=QT_BF_AT, align_bytes=64)
        nc.scalar.copy(
            qt_bf[:, 0 : SCALAR_QUERIES * PACK].rearrange("p (c i j) -> p c j i", i=4, j=PACK),
            qt_raw[0][:].rearrange("p j (c i) -> p c j i", i=4),
        )
        nc.gpsimd.tensor_scalar(
            qt_bf[:, SCALAR_QUERIES * PACK :].rearrange("p (c j) -> p c j", j=PACK),
            qt_raw[1][:].rearrange("p j c -> p c j"),
            1.0,
            0.0,
            mybir.AluOpType.mult,
            mybir.AluOpType.add,
        )

        dt_bf = {}
        for first, last in GROUPS:
            shape = [P, (last - first) * CHUNK * PACK]
            if first == 0:
                dt_bf[first] = shared.tile(shape, BF16, name="dt_bf0", offset=FIRST_DT_AT, align_bytes=64)
            else:
                dt_bf[first] = keep.tile(shape, BF16, name="dt_bf%d" % first, align_bytes=64)

        def empty_bank(c):
            first = max(g for g in dt_bf if g <= c)
            width = CHUNK * PACK
            rounded = dt_bf[first][:, (c - first) * width : (c - first + 1) * width].rearrange("p (n t) -> p n t", t=PACK)
            sums = banks[c][:].rearrange("p t n -> p n t")
            if c == VECTOR_CHUNK:
                nc.vector.tensor_copy(rounded, sums)
            elif c == SHARED_CHUNK:
                nc.vector.tensor_copy(rounded[:, 0:VECTOR_SLOTS], sums[:, 0:VECTOR_SLOTS])
                nc.scalar.copy(rounded[:, VECTOR_SLOTS:], sums[:, VECTOR_SLOTS:])
            else:
                nc.scalar.copy(rounded, sums)
            if c + PROJ_BANKS < CHUNKS:
                project(c + PROJ_BANKS)

        qt_codes = keep.tile([P, Q], U32, name="qt_codes", align_bytes=64)
        qt_plane = keep.tile([P, Q], U8, name="qt_plane", align_bytes=64)
        dt_codes = keep.tile([P, SLOTS], U32, name="dt_codes", align_bytes=64)
        dt_plane = keep.tile([P, SLOTS], U8, name="dt_plane", align_bytes=64)
        scores = {}

        def score(first, last):
            a, b = first * CHUNK, last * CHUNK
            scores[first] = score_banks.tile([P, 2, b - a], F32, name="score")
            for h in range(2):
                multiply(scores[first][:, h, :], qt_codes, qt_plane, h * P, dt_codes[:, a:b].bitcast(FP8X4), dt_plane[:, a:b])

        passages = CHUNK // RUN
        out_rows = out.rearrange("(h p) g -> p h g", h=2)
        best = {lo: keep.tile([P, 2, (hi - lo) * passages], F32, name="best%d" % lo, align_bytes=64) for lo, hi in STORES}

        def keep_best(first, last):
            lo, hi = [s for s in STORES if s[0] <= first < s[1]][0]
            nc.vector.tensor_reduce(
                best[lo][:, :, (first - lo) * passages : (last - lo) * passages],
                scores[first][:].rearrange("p h (g s) -> p h g s", s=RUN),
                mybir.AxisListType.X,
                mybir.AluOpType.max,
            )
            if last == hi:
                nc.sync.dma_start(out_rows[:, :, lo * passages : hi * passages], best[lo][:])

        quantize(qt_codes, qt_plane, 0, P, qt_bf[:, 0 : P * PACK])
        for c in range(SHARED_CHUNK + 1):
            empty_bank(c)

        waiting = []
        for first, last in GROUPS:
            for c in range(max(first, SHARED_CHUNK + 1), last):
                empty_bank(c)
            cuts = range(first, last + 1) if first > SHARED_CHUNK else (first, last)
            for a, b in zip(cuts, cuts[1:]):
                quantize(dt_codes, dt_plane, a * CHUNK, b * CHUNK, dt_bf[first][:, (a - first) * CHUNK * PACK : (b - first) * CHUNK * PACK])
            if first == 0:
                quantize(qt_codes, qt_plane, P, Q, qt_bf[:, P * PACK :])
            for group in [g for g in waiting if g[1] + MAX_LAG <= last]:
                keep_best(*group)
                waiting.remove(group)
            score(first, last)
            waiting.append((first, last))
        for group in waiting:
            keep_best(*group)
